import numpy as np, ml_dtypes
CORES = [76,84,92,100,108,116,124]
N = 7
import mx_ref
NC, W = 128, 6
BF = ml_dtypes.bfloat16
def cut(t, i, w=512):
    return t[:, w * i:w * i + w]
def term(a, B):
    return np.stack([mx_ref.matmul(mx_ref.quantize(cut(a, i)), B) for i in range(4)], axis=2).reshape(128, -1)
def setup_inputs(rng):
    def f(*shape):
        return mx_ref.flush((rng.standard_normal(shape, dtype=np.float32) * np.exp2(rng.integers(-2, 3, shape[:-1] + (1,)))).astype(BF))
    return {"a": f(N, 128, 4 * 512), "b": f(N, 128, 4 * NC)}
def setup_inputs_blocks(rng):
    d = setup_inputs(rng)
    for k in ("a", "b"): d[k] = mx_ref.spread(d[k], rng, 2)
    return d
def setup_inputs_wide(rng):
    d = setup_inputs(rng)
    for k in ("a", "b"): d[k] = mx_ref.flush((d[k].astype(np.float32) * np.exp2(rng.integers(-4, 5, (N, 1, 1))).astype(np.float32)).astype(BF))
    return d
def setup_inputs_lossless(rng):
    a = np.zeros((N, 128, 4 * 128, 4), np.float32)
    for r in range(N):
        k = rng.integers(0, 512, size=4 * 128)
        a[r, k // 4, np.arange(4 * 128), k % 4] = 1.0
    size = np.repeat(2.0 ** rng.integers(-4, 5, size=(1, 1, (4 * NC) // 4)), 4, axis=2)
    b = rng.integers(-1, 2, size=(N, 128, 4 * NC)) * size
    return {"a": a.reshape(N, 128, 4 * 512).astype(BF), "b": b.astype(np.float32).astype(BF)}
def reference(a, b):
    T = [term(a[r], mx_ref.quantize(b[r])) for r in range(N)]
    y = np.zeros((N, 128, 4 * NC), np.float32)
    for c in range(N):
        y[c] = mx_ref.total([T[(c - k) % N] for k in range(W)])
    return {"y": y}

@@ -1,0 +1,225 @@
+from concourse.bass import DstId, RemoteDMATransfer
+from concourse.mybir import dt, AluOpType, ActivationFunctionType
+
+N, W, NC = 7, 6, 128
+E = 4 * NC
+
+SCRATCH = {
+    "at": ("sbuf", [128, 4 * E], "bfloat16"), "bt": ("sbuf", [128, E], "bfloat16"),
+    "aq": ("sbuf", [128, 4 * NC], "float8_e4m3fn_x4"), "ap": ("sbuf", [128, 4 * NC], "uint8"),
+    "bq": ("sbuf", [128, NC], "float8_e4m3fn_x4"), "bp": ("sbuf", [128, NC], "uint8"),
+    "tt": ("sbuf", [128, E], "bfloat16"),
+    "tq": ("sbuf", [128, NC], "float8_e4m3fn_x4"), "tp": ("sbuf", [128, NC], "uint8"),
+    "sel": ("sbuf", [128, E + 8], "bfloat16"),
+    "wq": ("sbuf", [128, 4 * NC], "float8_e4m3fn_x4"), "wp": ("sbuf", [128, 4 * NC], "uint8"),
+    "ys": ("sbuf", [128, E], "float32"),
+    "ps": ("psum", [128, 8 * 512], "float32"),
+}
+TAGS = ["t%d" % r for r in range(N)] + ["P", "Q"]
+for _t in TAGS:
+    SCRATCH["q_" + _t] = ("sbuf", [128, NC], "float8_e4m3fn_x4")
+    SCRATCH["p_" + _t] = ("sbuf", [128, NC], "uint8")
+SEMAPHORES = (["in_" + t for t in TAGS] + ["lb", "la0", "la1", "qb", "zero", "one", "sel4", "evs", "evv", "qt", "out",
+              "ye", "st"] + ["qa%d" % i for i in range(4)] + ["m%d" % i for i in range(4)] + ["d%d" % i for i in range(4)])
+
+
+def _plan(cores, sim, topo):
+    chip = topo.chip
+    home = [r for r in range(N) if r == 0 or topo.same_plane(chip(cores[0]), chip(cores[r]))]
+    far = [r for r in range(N) if r not in home]
+    win = [set((c - k) % N for k in range(W)) for c in range(N)]
+    P = {x: set(home) - {x} for x in home}
+    Q = {x: win[x] & set(far) for x in home}
+    outs = {("P", x): [] for x in home}
+    outs.update({("Q", x): [] for x in home})
+    own = []
+    for c in range(N):
+        got = set()
+        for kind, part, plane in (("P", P, home), ("Q", Q, far)):
+            need = win[c] & set(plane)
+            fit = [x for x in home if x == c and need - {c} == part[x]]
+            fit += [x for x in home if need == part[x]] + [x for x in home if need - {c} == part[x]]
+            outs[(kind, fit[0])].append(c)
+            got |= part[fit[0]]
+        own.append(c not in got)
+    n_chips = 1 + max(chip(s) for s in range(sim))
+    comb = []
+    for (kind, x), dst in outs.items():
+        at = chip(cores[x])
+        if kind == "Q":
+            at = [k for k in range(n_chips) if topo.mates(k, at)][0]
+        core = [s for s in range(sim) if chip(s) == at and topo.die(s) == topo.die(cores[x]) and s not in cores
+                and all(topo.may_write(s, cores[d]) for d in dst)][0]
+        if kind == "P":
+            i = home.index(x)
+            ins = [home[(i - k) % len(home)] for k in range(1, len(home))]
+        else:
+            ins = sorted(Q[x], key=lambda r: chip(cores[r]) != at)
+        comb.append({"core": core, "ins": ins, "outs": dst, "kind": kind, "x": x})
+    return home, comb, own
+
+
+def rank_program(g, core, T, topo):
+    cores = list(T.cores)
+    sim = 128
+    home, comb, own = _plan(cores, sim, topo)
+    rank = T.rank_of(core)
+    mine = [k for k in comb if k["core"] == core]
+    if rank is None and not mine:
+        return
+    sem = T.sem
+    COPY = ActivationFunctionType.Copy
+
+    def bank(b):
+        return T.ps[:, 512 * b:512 * b + NC]
+
+    def dst_id(c):
+        a = topo.addr(c)
+        return DstId(rid=a[0], pnc=a[1])
+
+    sent = [0]
+
+    def send(tag, groups, planes):
+        src = T.tp[:] if planes else T.tq[:].bitcast(dt.uint8)
+        dst = T["p_" + tag][:] if planes else T["q_" + tag][:].bitcast(dt.uint8)
+        tr = []
+        for cs, mask in groups:
+            tr.append(RemoteDMATransfer(dst_ids=[dst_id(c) for c in cs], dma_engine_mask=mask,
+                                        remote_sem=sem["in_" + tag], srcs=[src], dsts=[dst for _ in cs]))
+            sent[0] += bin(mask).count("1")
+        g.remote_dma_fused(tr, local_sem=sem.out)
+
+    def split(dests):
+        on = [c for c in dests if topo.chip(c) == topo.chip(core)]
+        off = [c for c in dests if topo.chip(c) != topo.chip(core)]
+        m_off = topo.mask(core, off[0]) if off else 0
+        m_on = topo.mask(core, on[0]) & ~m_off if on else 0
+        return on, off, m_on, m_off
+
+    def decode(tag, base, start, stop, done=False):
+        g.tensor.wait_ge(sem["in_" + tag], got[tag])
+        for t in range(4):
+            s = slice(NC * t, NC * t + NC)
+            i = g.tensor.matmul_mx(bank(base + t), T.wq[:, s], T.wp[:, s], T["q_" + tag][:], T["p_" + tag][:], start, stop)
+            if done:
+                i.then_inc(sem["d%d" % t], 1)
+
+    def selectors():
+        g.vector.wait_ge(sem.one, 1)
+        for t in range(4):
+            s = slice(NC * t, NC * t + NC)
+            g.vector.quantize_mx(T.wq[:, s], T.wp[:, s], T.sel[:, 3 - t:3 - t + E]).then_inc(sem.sel4, 1)
+
+    got = {}
+    if rank is not None:
+        for k in comb:
+            if rank in k["outs"]:
+                m = topo.mask(k["core"], core)
+                if topo.chip(k["core"]) == topo.chip(core):
+                    offs = [cores[d] for d in k["outs"] if topo.chip(cores[d]) != topo.chip(core)]
+                    for o in offs[:1]:
+                        m &= ~topo.mask(k["core"], o)
+                got[k["kind"]] = 2 * bin(m).count("1")
+    for k in mine:
+        for r in k["ins"]:
+            m = topo.mask(cores[r], core)
+            if topo.chip(cores[r]) == topo.chip(core):
+                o = [j["core"] for j in comb if r in j["ins"] and topo.chip(j["core"]) != topo.chip(core)][0]
+                m &= ~topo.mask(cores[r], o)
+            got["t%d" % r] = 2 * bin(m).count("1")
+
+    g.vector.memset(T.sel[:], 0.0).then_inc(sem.zero, 1)
+    g.wait_ge(sem.zero, 1)
+    g.affine_select(T.sel[:], T.sel[:], [[1, E + 8]], AluOpType.not_equal, 1.0, -3, -4).then_inc(sem.one, 1)
+
+    if mine:
+        k = mine[0]
+        selectors()
+        g.tensor.wait_ge(sem.sel4, 4)
+        for i, r in enumerate(k["ins"]):
+            last = i == len(k["ins"]) - 1
+            decode("t%d" % r, 0, i == 0, last, last)
+        for t in (0, 2):
+            g.scalar.wait_ge(sem["d%d" % t], 1)
+            g.scalar.activation(T.tt[:, t:E:4], bank(t), COPY).then_inc(sem.evs, 1)
+        for t in (1, 3):
+            g.vector.wait_ge(sem["d%d" % t], 1)
+            g.vector.tensor_copy(T.tt[:, t:E:4], bank(t)).then_inc(sem.evv, 1)
+        g.vector.wait_ge(sem.evs, 2)
+        g.vector.wait_ge(sem.evv, 2)
+        g.vector.quantize_mx(T.tq[:], T.tp[:], T.tt[:]).then_inc(sem.qt, 1)
+        g.wait_ge(sem.qt, 1)
+        on, off, m_on, m_off = split([cores[d] for d in k["outs"]])
+        groups = ([(off, m_off)] if off else []) + ([(on, m_on)] if on else [])
+        send(k["kind"], groups, True)
+        send(k["kind"], groups, False)
+        g.wait_ge(sem.out, sent[0])
+        return
+
+    half = 2 * E
+    g.sync.dma_start(T.bt[:], T.b[:]).then_inc(sem.lb, 16)
+    g.scalar.dma_start(T.at[:, 0:half], T.a[:, 0:half]).then_inc(sem.la0, 16)
+    g.sync.dma_start(T.at[:, half:2 * half], T.a[:, half:2 * half]).then_inc(sem.la1, 16)
+
+    g.vector.wait_ge(sem.lb, 16)
+    g.vector.quantize_mx(T.bq[:], T.bp[:], T.bt[:]).then_inc(sem.qb, 1)
+    for i in range(4):
+        if i % 2 == 0:
+            g.vector.wait_ge(sem["la%d" % (i // 2)], 16)
+        s = slice(NC * i, NC * i + NC)
+        g.vector.quantize_mx(T.aq[:, s], T.ap[:, s], T.at[:, E * i:E * i + E]).then_inc(sem["qa%d" % i], 1)
+
+    def product(i, b, start, stop):
+        s = slice(NC * i, NC * i + NC)
+        return g.tensor.matmul_mx(bank(b), T.aq[:, s], T.ap[:, s], T.bq[:], T.bp[:], start, stop)
+
+    g.tensor.wait_ge(sem.qb, 1)
+    for i in range(4):
+        g.tensor.wait_ge(sem["qa%d" % i], 1)
+        product(i, i, True, True).then_inc(sem["m%d" % i], 1)
+
+    for i in range(3):
+        g.scalar.wait_ge(sem["m%d" % i], 1)
+        g.scalar.activation(T.tt[:, i:E:4], bank(i), COPY).then_inc(sem.evs, 1)
+    g.vector.wait_ge(sem.m3, 1)
+    g.vector.tensor_copy(T.tt[:, 3:E:4], bank(3)).then_inc(sem.evv, 1)
+    g.vector.wait_ge(sem.evs, 3)
+    g.vector.wait_ge(sem.evv, 1)
+    g.vector.quantize_mx(T.tq[:], T.tp[:], T.tt[:]).then_inc(sem.qt, 1)
+
+    tag = "t%d" % rank
+    if rank in home:
+        i = home.index(rank)
+        order = [home[(i + k) % len(home)] for k in range(1, len(home))]
+        dests = [j["core"] for x in order for j in comb if j["kind"] == "P" and j["x"] == x]
+    else:
+        dests = [j["core"] for j in comb if rank in j["ins"]]
+    on, off, m_on, m_off = split(dests)
+    g.wait_ge(sem.qt, 1)
+    send(tag, [(off, m_off)], True)
+    if rank in home:
+        for d in off:
+            send(tag, [([d], m_off)], False)
+    else:
+        send(tag, [(off, m_off)], False)
+    if on:
+        send(tag, [(on, m_on)], True)
+        send(tag, [(on, m_on)], False)
+
+    selectors()
+    if own[rank]:
+        for i in range(4):
+            product(i, 4 + i, True, False)
+    g.tensor.wait_ge(sem.sel4, 4)
+    decode("Q", 4, not own[rank], False)
+    decode("P", 4, False, True, True)
+    for t in (0, 2):
+        g.scalar.wait_ge(sem["d%d" % t], 1)
+        g.scalar.activation(T.ys[:, t:E:4], bank(4 + t), COPY).then_inc(sem.ye, 1)
+    for t in (1, 3):
+        g.vector.wait_ge(sem["d%d" % t], 1)
+        g.vector.tensor_copy(T.ys[:, t:E:4], bank(4 + t)).then_inc(sem.ye, 1)
+    g.sync.wait_ge(sem.ye, 4)
+    g.sync.dma_start(T.y[:], T.ys[:]).then_inc(sem.st, 16)
+    g.sync.wait_ge(sem.st, 16)
+    g.wait_ge(sem.out, sent[0])

@@ -4,71 +4,69 @@ from concourse.mybir import dt, AluOpType, ActivationFunctionType
 N, W, NC = 7, 6, 128
 E = 4 * NC
 
-SCRATCH = {
-    "at": ("sbuf", [128, 4 * E], "bfloat16"), "bt": ("sbuf", [128, E], "bfloat16"),
-    "aq": ("sbuf", [128, 4 * NC], "float8_e4m3fn_x4"), "ap": ("sbuf", [128, 4 * NC], "uint8"),
-    "bq": ("sbuf", [128, NC], "float8_e4m3fn_x4"), "bp": ("sbuf", [128, NC], "uint8"),
-    "tt": ("sbuf", [128, E], "bfloat16"),
-    "tq": ("sbuf", [128, NC], "float8_e4m3fn_x4"), "tp": ("sbuf", [128, NC], "uint8"),
-    "sel": ("sbuf", [128, E + 8], "bfloat16"),
-    "wq": ("sbuf", [128, 4 * NC], "float8_e4m3fn_x4"), "wp": ("sbuf", [128, 4 * NC], "uint8"),
-    "ys": ("sbuf", [128, E], "float32"),
-    "ps": ("psum", [128, 8 * 512], "float32"),
+HELP = {
+    "A0": (0, "own", [4, 2], None, [[("t6", "t6", [0])], [("x0", "S", [0])]]),
+    "A2": (2, "own", [6, 4], 0, [[("t0", "t0", [2])], [("x1", "S", [1])], [("x0", "S", [2])]]),
+    "A4": (4, "own", [0, 6], 2, [[("t2", "t2", [4])], [("x1", "S", [3])], [("x0", "S", [4])]]),
+    "A6": (6, "own", [4, 2, 0], None, [[("t4", "t4", [6])], [("t2", "t2", [6])], [("x0", "S", [5])]]),
+    "C0": (0, "mate", [5, 3], None, [[("t3", "t3", [1])], [("x0", "Q", [0])]]),
+    "B1": (1, "own", [1, 5], None, [[("t5", "t5", [1])], [("x0", "Q", [2])]]),
+    "B3": (3, "own", [3, 1], None, [[("t1", "t1", [3])], [("x0", "Q", [4])]]),
+    "B5": (5, "own", [5, 1, 3], None, [[("t1", "t1", [5])], [("x0", "Q", [6])]]),
 }
-TAGS = ["t%d" % r for r in range(N)] + ["P", "Q"]
-for _t in TAGS:
-    SCRATCH["q_" + _t] = ("sbuf", [128, NC], "float8_e4m3fn_x4")
-    SCRATCH["p_" + _t] = ("sbuf", [128, NC], "uint8")
-SEMAPHORES = (["in_" + t for t in TAGS] + ["lb", "la0", "la1", "qb", "zero", "one", "sel4", "evs", "evv", "qt", "out",
-              "ye", "st"] + ["qa%d" % i for i in range(4)] + ["m%d" % i for i in range(4)] + ["d%d" % i for i in range(4)])
+HOP1 = [
+    [[["A2", "A4", "A6"], ["A2"], ["A4"], ["A6"]]],
+    [[["B5", "B3"], ["B5", "B3"]], [["B1"], ["B1"]]],
+    [[["A4", "A6", "A0"], ["A4"], ["A6"], ["A0"]]],
+    [[["C0", "B5"], ["C0", "B5"]], [["B3"], ["B3"]], [[5], [5]]],
+    [[["A6", "A0", "A2"], ["A6"], ["A0"], ["A2"]]],
+    [[["B1", "C0"], ["B1", "C0"]], [["B5"], ["B5"]], [[3], [3]]],
+    [[["A0", "A2", "A4"], ["A0"], ["A2"], ["A4"]]],
+]
+LAND = [["t6", "S", "Q"], ["t5", "t3", "S"], ["t0", "Q", "S"], ["t5", "t1", "S"], ["t2", "Q", "S"], ["t3", "t1", "S"],
+        ["t4", "t2", "Q"]]
+
+BF, F8, U8 = "bfloat16", "float8_e4m3fn_x4", "uint8"
+SCRATCH = {
+    "at": ("sbuf", [128, 4 * E], BF), "bt": ("sbuf", [128, E], BF),
+    "aq": ("sbuf", [128, 4 * NC], F8), "ap": ("sbuf", [128, 4 * NC], U8),
+    "bq": ("sbuf", [128, NC], F8), "bp": ("sbuf", [128, NC], U8),
+    "sel": ("sbuf", [128, E + 8], BF),
+    "wq": ("sbuf", [128, 4 * NC], F8), "wp": ("sbuf", [128, 4 * NC], U8),
+    "xa": ("sbuf", [128, E], "float32"), "ys": ("sbuf", [128, E], "float32"),
+    "ps": ("psum", [128, 8 * 512], "float32"),
+    "x0": ("sbuf", [128, E], BF), "x1": ("sbuf", [128, E], BF),
+}
+TAGS = ["t%d" % r for r in range(N)] + ["S", "Q"]
+for _t in TAGS + ["x0", "x1"]:
+    SCRATCH["q_" + _t] = ("sbuf", [128, NC], F8)
+    SCRATCH["p_" + _t] = ("sbuf", [128, NC], U8)
+SEMAPHORES = (["in_" + t for t in TAGS] + ["lb", "la0", "la1", "qb", "zero", "one", "sel4", "out", "ye", "st", "qt_x0", "qt_x1"]
+              + [k + str(i) for k in ("qa", "m", "v", "w", "u", "h") for i in range(4)] + ["d%d" % i for i in range(8)])
 
 
-def _plan(cores, sim, topo):
-    chip = topo.chip
-    home = [r for r in range(N) if r == 0 or topo.same_plane(chip(cores[0]), chip(cores[r]))]
-    far = [r for r in range(N) if r not in home]
-    win = [set((c - k) % N for k in range(W)) for c in range(N)]
-    P = {x: set(home) - {x} for x in home}
-    Q = {x: win[x] & set(far) for x in home}
-    outs = {("P", x): [] for x in home}
-    outs.update({("Q", x): [] for x in home})
-    own = []
-    for c in range(N):
-        got = set()
-        for kind, part, plane in (("P", P, home), ("Q", Q, far)):
-            need = win[c] & set(plane)
-            fit = [x for x in home if x == c and need - {c} == part[x]]
-            fit += [x for x in home if need == part[x]] + [x for x in home if need - {c} == part[x]]
-            outs[(kind, fit[0])].append(c)
-            got |= part[fit[0]]
-        own.append(c not in got)
-    n_chips = 1 + max(chip(s) for s in range(sim))
-    comb = []
-    for (kind, x), dst in outs.items():
-        at = chip(cores[x])
-        if kind == "Q":
-            at = [k for k in range(n_chips) if topo.mates(k, at)][0]
-        core = [s for s in range(sim) if chip(s) == at and topo.die(s) == topo.die(cores[x]) and s not in cores
-                and all(topo.may_write(s, cores[d]) for d in dst)][0]
-        if kind == "P":
-            i = home.index(x)
-            ins = [home[(i - k) % len(home)] for k in range(1, len(home))]
-        else:
-            ins = sorted(Q[x], key=lambda r: chip(cores[r]) != at)
-        comb.append({"core": core, "ins": ins, "outs": dst, "kind": kind, "x": x})
-    return home, comb, own
+def _place(name, cores, sim, topo):
+    rank, where = HELP[name][:2]
+    me = cores[rank]
+    chip = topo.chip(me)
+    if where == "mate":
+        chip = [topo.chip(s) for s in range(sim) if topo.mates(topo.chip(s), chip)][0]
+    return [s for s in range(sim) if topo.chip(s) == chip and topo.die(s) == topo.die(me) and s not in cores
+            and all(topo.may_write(s, c) for c in range(sim))][0]
 
 
 def rank_program(g, core, T, topo):
     cores = list(T.cores)
-    sim = 128
-    home, comb, own = _plan(cores, sim, topo)
+    place = {n: _place(n, cores, 128, topo) for n in HELP}
     rank = T.rank_of(core)
-    mine = [k for k in comb if k["core"] == core]
-    if rank is None and not mine:
+    names = [n for n in HELP if place[n] == core]
+    if rank is None and not names:
         return
     sem = T.sem
     COPY = ActivationFunctionType.Copy
+
+    def at(d):
+        return place[d] if d in place else cores[d]
 
     def bank(b):
         return T.ps[:, 512 * b:512 * b + NC]
@@ -77,32 +75,68 @@ def rank_program(g, core, T, topo):
         a = topo.addr(c)
         return DstId(rid=a[0], pnc=a[1])
 
+    def engines(src, dst, tag):
+        m = topo.mask(src, dst)
+        if topo.chip(src) == topo.chip(dst):
+            low = topo.mask(src, [c for c in cores if topo.chip(c) != topo.chip(src)][0])
+            early = tag[0] == "t" and any(place[n] == src and n[0] == "A" for n in HELP)
+            m = low if early else m & ~low
+        return m
+
     sent = [0]
 
-    def send(tag, groups, planes):
-        src = T.tp[:] if planes else T.tq[:].bitcast(dt.uint8)
-        dst = T["p_" + tag][:] if planes else T["q_" + tag][:].bitcast(dt.uint8)
+    def send(pq, tiles):
         tr = []
-        for cs, mask in groups:
-            tr.append(RemoteDMATransfer(dst_ids=[dst_id(c) for c in cs], dma_engine_mask=mask,
-                                        remote_sem=sem["in_" + tag], srcs=[src], dsts=[dst for _ in cs]))
+        for what, tag, dests in tiles:
+            src, dst = T[pq + "_" + what][:], T[pq + "_" + tag][:]
+            if pq == "q":
+                src, dst = src.bitcast(dt.uint8), dst.bitcast(dt.uint8)
+            mask = engines(core, dests[0], tag)
+            tr.append(RemoteDMATransfer(dst_ids=[dst_id(c) for c in dests], dma_engine_mask=mask,
+                                        remote_sem=sem["in_" + tag], srcs=[src], dsts=[dst for _ in dests]))
             sent[0] += bin(mask).count("1")
         g.remote_dma_fused(tr, local_sem=sem.out)
 
-    def split(dests):
-        on = [c for c in dests if topo.chip(c) == topo.chip(core)]
-        off = [c for c in dests if topo.chip(c) != topo.chip(core)]
-        m_off = topo.mask(core, off[0]) if off else 0
-        m_on = topo.mask(core, on[0]) & ~m_off if on else 0
-        return on, off, m_on, m_off
+    def source(tag):
+        if rank is not None:
+            for n, h in HELP.items():
+                for call in h[4]:
+                    for what, t, outs in call:
+                        if rank in outs and t == tag:
+                            return place[n]
+        return cores[int(tag[1:])]
 
-    def decode(tag, base, start, stop, done=False):
-        g.tensor.wait_ge(sem["in_" + tag], got[tag])
+    def arrive(queue, tag):
+        queue.wait_ge(sem["in_" + tag], 2 * bin(engines(source(tag), core, tag)).count("1"))
+
+    def decode(tag, base, start, stop):
+        arrive(g.tensor, tag)
         for t in range(4):
             s = slice(NC * t, NC * t + NC)
             i = g.tensor.matmul_mx(bank(base + t), T.wq[:, s], T.wp[:, s], T["q_" + tag][:], T["p_" + tag][:], start, stop)
-            if done:
-                i.then_inc(sem["d%d" % t], 1)
+            if stop:
+                i.then_inc(sem["d%d" % (base + t)], 1)
+
+    def cols(t):
+        return slice(t, E, 4)
+
+    def drain(buf, base, where, out):
+        for t in (0, 2):
+            g.scalar.wait_ge(sem["d%d" % (base + t)], 1)
+            g.scalar.activation(buf[:, where(t)], bank(base + t), COPY).then_inc(sem[out[t]], 1)
+        for t in (1, 3):
+            g.vector.wait_ge(sem["d%d" % (base + t)], 1)
+            g.vector.tensor_copy(buf[:, where(t)], bank(base + t)).then_inc(sem[out[t]], 1)
+
+    def pack(x, done):
+        for t in range(4):
+            g.vector.wait_ge(sem["%s%d" % (done, t)], 1)
+        g.vector.quantize_mx(T["q_" + x][:], T["p_" + x][:], T[x][:]).then_inc(sem["qt_" + x], 1)
+
+    def diagonal():
+        g.vector.memset(T.sel[:], 0.0).then_inc(sem.zero, 1)
+        g.wait_ge(sem.zero, 1)
+        g.affine_select(T.sel[:], T.sel[:], [[1, E + 8]], AluOpType.not_equal, 1.0, -3, -4).then_inc(sem.one, 1)
 
     def selectors():
         g.vector.wait_ge(sem.one, 1)
@@ -110,52 +144,40 @@ def rank_program(g, core, T, topo):
             s = slice(NC * t, NC * t + NC)
             g.vector.quantize_mx(T.wq[:, s], T.wp[:, s], T.sel[:, 3 - t:3 - t + E]).then_inc(sem.sel4, 1)
 
-    got = {}
-    if rank is not None:
-        for k in comb:
-            if rank in k["outs"]:
-                m = topo.mask(k["core"], core)
-                if topo.chip(k["core"]) == topo.chip(core):
-                    offs = [cores[d] for d in k["outs"] if topo.chip(cores[d]) != topo.chip(core)]
-                    for o in offs[:1]:
-                        m &= ~topo.mask(k["core"], o)
-                got[k["kind"]] = 2 * bin(m).count("1")
-    for k in mine:
-        for r in k["ins"]:
-            m = topo.mask(cores[r], core)
-            if topo.chip(cores[r]) == topo.chip(core):
-                o = [j["core"] for j in comb if r in j["ins"] and topo.chip(j["core"]) != topo.chip(core)][0]
-                m &= ~topo.mask(cores[r], o)
-            got["t%d" % r] = 2 * bin(m).count("1")
-
-    g.vector.memset(T.sel[:], 0.0).then_inc(sem.zero, 1)
-    g.wait_ge(sem.zero, 1)
-    g.affine_select(T.sel[:], T.sel[:], [[1, E + 8]], AluOpType.not_equal, 1.0, -3, -4).then_inc(sem.one, 1)
-
-    if mine:
-        k = mine[0]
+    if names:
+        terms, more, calls = HELP[names[0]][2:]
+        diagonal()
         selectors()
         g.tensor.wait_ge(sem.sel4, 4)
-        for i, r in enumerate(k["ins"]):
-            last = i == len(k["ins"]) - 1
-            decode("t%d" % r, 0, i == 0, last, last)
-        for t in (0, 2):
-            g.scalar.wait_ge(sem["d%d" % t], 1)
-            g.scalar.activation(T.tt[:, t:E:4], bank(t), COPY).then_inc(sem.evs, 1)
-        for t in (1, 3):
-            g.vector.wait_ge(sem["d%d" % t], 1)
-            g.vector.tensor_copy(T.tt[:, t:E:4], bank(t)).then_inc(sem.evv, 1)
-        g.vector.wait_ge(sem.evs, 2)
-        g.vector.wait_ge(sem.evv, 2)
-        g.vector.quantize_mx(T.tq[:], T.tp[:], T.tt[:]).then_inc(sem.qt, 1)
-        g.wait_ge(sem.qt, 1)
-        on, off, m_on, m_off = split([cores[d] for d in k["outs"]])
-        groups = ([(off, m_off)] if off else []) + ([(on, m_on)] if on else [])
-        send(k["kind"], groups, True)
-        send(k["kind"], groups, False)
+        if more is not None:
+            decode("t%d" % more, 4, True, True)
+            drain(T.xa, 4, lambda t: slice(NC * t, NC * t + NC), ["u%d" % t for t in range(4)])
+        for i, r in enumerate(terms):
+            decode("t%d" % r, 0, i == 0, i == len(terms) - 1)
+        if more is None:
+            drain(T.x0, 0, cols, ["w%d" % t for t in range(4)])
+        else:
+            for t in range(4):
+                g.vector.wait_ge(sem["u%d" % t], 1)
+            for t in range(4):
+                g.vector.wait_ge(sem["d%d" % t], 1)
+                g.vector.tensor_tensor(T.x1[:, cols(t)], bank(t), T.xa[:, NC * t:NC * t + NC], AluOpType.add).then_inc(sem["h%d" % t], 1)
+                g.scalar.wait_ge(sem["h%d" % t], 1)
+                g.scalar.activation(T.x0[:, cols(t)], bank(t), COPY).then_inc(sem["w%d" % t], 1)
+            pack("x1", "h")
+        pack("x0", "w")
+        for call in calls:
+            for what, tag, outs in call:
+                if what[0] == "t":
+                    arrive(g, what)
+                else:
+                    g.wait_ge(sem["qt_" + what], 1)
+            for pq in "pq":
+                send(pq, [(what, tag, [cores[c] for c in outs]) for what, tag, outs in call])
         g.wait_ge(sem.out, sent[0])
         return
 
+    diagonal()
     half = 2 * E
     g.sync.dma_start(T.bt[:], T.b[:]).then_inc(sem.lb, 16)
     g.scalar.dma_start(T.at[:, 0:half], T.a[:, 0:half]).then_inc(sem.la0, 16)
@@ -180,45 +202,23 @@ def rank_program(g, core, T, topo):
 
     for i in range(3):
         g.scalar.wait_ge(sem["m%d" % i], 1)
-        g.scalar.activation(T.tt[:, i:E:4], bank(i), COPY).then_inc(sem.evs, 1)
+        g.scalar.activation(T.x0[:, cols(i)], bank(i), COPY).then_inc(sem["v%d" % i], 1)
     g.vector.wait_ge(sem.m3, 1)
-    g.vector.tensor_copy(T.tt[:, 3:E:4], bank(3)).then_inc(sem.evv, 1)
-    g.vector.wait_ge(sem.evs, 3)
-    g.vector.wait_ge(sem.evv, 1)
-    g.vector.quantize_mx(T.tq[:], T.tp[:], T.tt[:]).then_inc(sem.qt, 1)
+    g.vector.tensor_copy(T.x0[:, cols(3)], bank(3)).then_inc(sem.v3, 1)
+    pack("x0", "v")
 
-    tag = "t%d" % rank
-    if rank in home:
-        i = home.index(rank)
-        order = [home[(i + k) % len(home)] for k in range(1, len(home))]
-        dests = [j["core"] for x in order for j in comb if j["kind"] == "P" and j["x"] == x]
-    else:
-        dests = [j["core"] for j in comb if rank in j["ins"]]
-    on, off, m_on, m_off = split(dests)
-    g.wait_ge(sem.qt, 1)
-    send(tag, [(off, m_off)], True)
-    if rank in home:
-        for d in off:
-            send(tag, [([d], m_off)], False)
-    else:
-        send(tag, [(off, m_off)], False)
-    if on:
-        send(tag, [(on, m_on)], True)
-        send(tag, [(on, m_on)], False)
+    g.wait_ge(sem.qt_x0, 1)
+    for calls in HOP1[rank]:
+        for n, dests in enumerate(calls):
+            send("p" if n == 0 else "q", [("x0", "t%d" % rank, [at(d) for d in dests])])
 
     selectors()
-    if own[rank]:
-        for i in range(4):
-            product(i, 4 + i, True, False)
+    for i in range(4):
+        product(i, 4 + i, True, False)
     g.tensor.wait_ge(sem.sel4, 4)
-    decode("Q", 4, not own[rank], False)
-    decode("P", 4, False, True, True)
-    for t in (0, 2):
-        g.scalar.wait_ge(sem["d%d" % t], 1)
-        g.scalar.activation(T.ys[:, t:E:4], bank(4 + t), COPY).then_inc(sem.ye, 1)
-    for t in (1, 3):
-        g.vector.wait_ge(sem["d%d" % t], 1)
-        g.vector.tensor_copy(T.ys[:, t:E:4], bank(4 + t)).then_inc(sem.ye, 1)
+    for n, tag in enumerate(LAND[rank]):
+        decode(tag, 4, False, n == len(LAND[rank]) - 1)
+    drain(T.ys, 4, cols, ["ye"] * 4)
     g.sync.wait_ge(sem.ye, 4)
     g.sync.dma_start(T.y[:], T.ys[:]).then_inc(sem.st, 16)
     g.sync.wait_ge(sem.st, 16)

from concourse.bass import DstId, RemoteDMATransfer
from concourse.mybir import dt, AluOpType, ActivationFunctionType

N, W, NC = 7, 6, 128
E = 4 * NC

HELP = {
    "A0": (0, "own", [4, 2], None, [[("t6", "t6", [0])], [("x0", "S", [0])]]),
    "A2": (2, "own", [6, 4], 0, [[("t0", "t0", [2])], [("x1", "S", [1])], [("x0", "S", [2])]]),
    "A4": (4, "own", [0, 6], 2, [[("t2", "t2", [4])], [("x1", "S", [3])], [("x0", "S", [4])]]),
    "A6": (6, "own", [4, 2, 0], None, [[("t4", "t4", [6])], [("t2", "t2", [6])], [("x0", "S", [5])]]),
    "C0": (0, "mate", [5, 3], None, [[("t3", "t3", [1])], [("x0", "Q", [0])]]),
    "B1": (1, "own", [1, 5], None, [[("t5", "t5", [1])], [("x0", "Q", [2])]]),
    "B3": (3, "own", [3, 1], None, [[("t1", "t1", [3])], [("x0", "Q", [4])]]),
    "B5": (5, "own", [5, 1, 3], None, [[("t1", "t1", [5])], [("x0", "Q", [6])]]),
}
HOP1 = [
    [[["A2", "A4", "A6"], ["A2"], ["A4"], ["A6"]]],
    [[["B5", "B3"], ["B5", "B3"]], [["B1"], ["B1"]]],
    [[["A4", "A6", "A0"], ["A4"], ["A6"], ["A0"]]],
    [[["C0", "B5"], ["C0", "B5"]], [["B3"], ["B3"]], [[5], [5]]],
    [[["A6", "A0", "A2"], ["A6"], ["A0"], ["A2"]]],
    [[["B1", "C0"], ["B1", "C0"]], [["B5"], ["B5"]], [[3], [3]]],
    [[["A0", "A2", "A4"], ["A0"], ["A2"], ["A4"]]],
]
LAND = [["t6", "S", "Q"], ["t5", "t3", "S"], ["t0", "Q", "S"], ["t5", "t1", "S"], ["t2", "Q", "S"], ["t3", "t1", "S"],
        ["t4", "t2", "Q"]]

BF, F8, U8 = "bfloat16", "float8_e4m3fn_x4", "uint8"
SCRATCH = {
    "at": ("sbuf", [128, 4 * E], BF), "bt": ("sbuf", [128, E], BF),
    "aq": ("sbuf", [128, 4 * NC], F8), "ap": ("sbuf", [128, 4 * NC], U8),
    "bq": ("sbuf", [128, NC], F8), "bp": ("sbuf", [128, NC], U8),
    "sel": ("sbuf", [128, E + 8], BF),
    "wq": ("sbuf", [128, 4 * NC], F8), "wp": ("sbuf", [128, 4 * NC], U8),
    "xa": ("sbuf", [128, E], "float32"), "ys": ("sbuf", [128, E], "float32"),
    "ps": ("psum", [128, 8 * 512], "float32"),
    "x0": ("sbuf", [128, E], BF), "x1": ("sbuf", [128, E], BF),
}
TAGS = ["t%d" % r for r in range(N)] + ["S", "Q"]
for _t in TAGS + ["x0", "x1"]:
    SCRATCH["q_" + _t] = ("sbuf", [128, NC], F8)
    SCRATCH["p_" + _t] = ("sbuf", [128, NC], U8)
SEMAPHORES = (["in_" + t for t in TAGS] + ["lb", "la0", "la1", "qb", "zero", "one", "sel4", "out", "ye", "st", "qt_x0", "qt_x1"]
              + [k + str(i) for k in ("qa", "m", "v", "w", "u", "h") for i in range(4)] + ["d%d" % i for i in range(8)])


def _place(name, cores, sim, topo):
    rank, where = HELP[name][:2]
    me = cores[rank]
    chip = topo.chip(me)
    if where == "mate":
        chip = [topo.chip(s) for s in range(sim) if topo.mates(topo.chip(s), chip)][0]
    return [s for s in range(sim) if topo.chip(s) == chip and topo.die(s) == topo.die(me) and s not in cores
            and all(topo.may_write(s, c) for c in range(sim))][0]


def rank_program(g, core, T, topo):
    cores = list(T.cores)
    place = {n: _place(n, cores, 128, topo) for n in HELP}
    rank = T.rank_of(core)
    names = [n for n in HELP if place[n] == core]
    if rank is None and not names:
        return
    sem = T.sem
    COPY = ActivationFunctionType.Copy

    def at(d):
        return place[d] if d in place else cores[d]

    def bank(b):
        return T.ps[:, 512 * b:512 * b + NC]

    def dst_id(c):
        a = topo.addr(c)
        return DstId(rid=a[0], pnc=a[1])

    def engines(src, dst, tag):
        m = topo.mask(src, dst)
        if topo.chip(src) == topo.chip(dst):
            low = topo.mask(src, [c for c in cores if topo.chip(c) != topo.chip(src)][0])
            early = tag[0] == "t" and any(place[n] == src and n[0] == "A" for n in HELP)
            m = low if early else m & ~low
        return m

    sent = [0]

    def send(pq, tiles):
        tr = []
        for what, tag, dests in tiles:
            src, dst = T[pq + "_" + what][:], T[pq + "_" + tag][:]
            if pq == "q":
                src, dst = src.bitcast(dt.uint8), dst.bitcast(dt.uint8)
            mask = engines(core, dests[0], tag)
            tr.append(RemoteDMATransfer(dst_ids=[dst_id(c) for c in dests], dma_engine_mask=mask,
                                        remote_sem=sem["in_" + tag], srcs=[src], dsts=[dst for _ in dests]))
            sent[0] += bin(mask).count("1")
        g.remote_dma_fused(tr, local_sem=sem.out)

    def source(tag):
        if rank is not None:
            for n, h in HELP.items():
                for call in h[4]:
                    for what, t, outs in call:
                        if rank in outs and t == tag:
                            return place[n]
        return cores[int(tag[1:])]

    def arrive(queue, tag):
        queue.wait_ge(sem["in_" + tag], 2 * bin(engines(source(tag), core, tag)).count("1"))

    def decode(tag, base, start, stop):
        arrive(g.tensor, tag)
        for t in range(4):
            s = slice(NC * t, NC * t + NC)
            i = g.tensor.matmul_mx(bank(base + t), T.wq[:, s], T.wp[:, s], T["q_" + tag][:], T["p_" + tag][:], start, stop)
            if stop:
                i.then_inc(sem["d%d" % (base + t)], 1)

    def cols(t):
        return slice(t, E, 4)

    def drain(buf, base, where, out):
        for t in (0, 2):
            g.scalar.wait_ge(sem["d%d" % (base + t)], 1)
            g.scalar.activation(buf[:, where(t)], bank(base + t), COPY).then_inc(sem[out[t]], 1)
        for t in (1, 3):
            g.vector.wait_ge(sem["d%d" % (base + t)], 1)
            g.vector.tensor_copy(buf[:, where(t)], bank(base + t)).then_inc(sem[out[t]], 1)

    def pack(x, done):
        for t in range(4):
            g.vector.wait_ge(sem["%s%d" % (done, t)], 1)
        g.vector.quantize_mx(T["q_" + x][:], T["p_" + x][:], T[x][:]).then_inc(sem["qt_" + x], 1)

    def diagonal():
        g.vector.memset(T.sel[:], 0.0).then_inc(sem.zero, 1)
        g.wait_ge(sem.zero, 1)
        g.affine_select(T.sel[:], T.sel[:], [[1, E + 8]], AluOpType.not_equal, 1.0, -3, -4).then_inc(sem.one, 1)

    def selectors():
        g.vector.wait_ge(sem.one, 1)
        for t in range(4):
            s = slice(NC * t, NC * t + NC)
            g.vector.quantize_mx(T.wq[:, s], T.wp[:, s], T.sel[:, 3 - t:3 - t + E]).then_inc(sem.sel4, 1)

    if names:
        terms, more, calls = HELP[names[0]][2:]
        diagonal()
        selectors()
        g.tensor.wait_ge(sem.sel4, 4)
        if more is not None:
            decode("t%d" % more, 4, True, True)
            drain(T.xa, 4, lambda t: slice(NC * t, NC * t + NC), ["u%d" % t for t in range(4)])
        for i, r in enumerate(terms):
            decode("t%d" % r, 0, i == 0, i == len(terms) - 1)
        if more is None:
            drain(T.x0, 0, cols, ["w%d" % t for t in range(4)])
        else:
            for t in range(4):
                g.vector.wait_ge(sem["u%d" % t], 1)
            for t in range(4):
                g.vector.wait_ge(sem["d%d" % t], 1)
                g.vector.tensor_tensor(T.x1[:, cols(t)], bank(t), T.xa[:, NC * t:NC * t + NC], AluOpType.add).then_inc(sem["h%d" % t], 1)
                g.scalar.wait_ge(sem["h%d" % t], 1)
                g.scalar.activation(T.x0[:, cols(t)], bank(t), COPY).then_inc(sem["w%d" % t], 1)
            pack("x1", "h")
        pack("x0", "w")
        for call in calls:
            for what, tag, outs in call:
                if what[0] == "t":
                    arrive(g, what)
                else:
                    g.wait_ge(sem["qt_" + what], 1)
            for pq in "pq":
                send(pq, [(what, tag, [cores[c] for c in outs]) for what, tag, outs in call])
        g.wait_ge(sem.out, sent[0])
        return

    diagonal()
    half = 2 * E
    g.sync.dma_start(T.bt[:], T.b[:]).then_inc(sem.lb, 16)
    g.scalar.dma_start(T.at[:, 0:half], T.a[:, 0:half]).then_inc(sem.la0, 16)
    g.sync.dma_start(T.at[:, half:2 * half], T.a[:, half:2 * half]).then_inc(sem.la1, 16)

    g.vector.wait_ge(sem.lb, 16)
    g.vector.quantize_mx(T.bq[:], T.bp[:], T.bt[:]).then_inc(sem.qb, 1)
    for i in range(4):
        if i % 2 == 0:
            g.vector.wait_ge(sem["la%d" % (i // 2)], 16)
        s = slice(NC * i, NC * i + NC)
        g.vector.quantize_mx(T.aq[:, s], T.ap[:, s], T.at[:, E * i:E * i + E]).then_inc(sem["qa%d" % i], 1)

    def product(i, b, start, stop):
        s = slice(NC * i, NC * i + NC)
        return g.tensor.matmul_mx(bank(b), T.aq[:, s], T.ap[:, s], T.bq[:], T.bp[:], start, stop)

    g.tensor.wait_ge(sem.qb, 1)
    for i in range(4):
        g.tensor.wait_ge(sem["qa%d" % i], 1)
        product(i, i, True, True).then_inc(sem["m%d" % i], 1)

    for i in range(3):
        g.scalar.wait_ge(sem["m%d" % i], 1)
        g.scalar.activation(T.x0[:, cols(i)], bank(i), COPY).then_inc(sem["v%d" % i], 1)
    g.vector.wait_ge(sem.m3, 1)
    g.vector.tensor_copy(T.x0[:, cols(3)], bank(3)).then_inc(sem.v3, 1)
    pack("x0", "v")

    g.wait_ge(sem.qt_x0, 1)
    for calls in HOP1[rank]:
        for n, dests in enumerate(calls):
            send("p" if n == 0 else "q", [("x0", "t%d" % rank, [at(d) for d in dests])])

    selectors()
    for i in range(4):
        product(i, 4 + i, True, False)
    g.tensor.wait_ge(sem.sel4, 4)
    for n, tag in enumerate(LAND[rank]):
        decode(tag, 4, False, n == len(LAND[rank]) - 1)
    drain(T.ys, 4, cols, ["ye"] * 4)
    g.sync.wait_ge(sem.ye, 4)
    g.sync.dma_start(T.y[:], T.ys[:]).then_inc(sem.st, 16)
    g.sync.wait_ge(sem.st, 16)
    g.wait_ge(sem.out, sent[0])
